import numpy as np
import ml_dtypes


def mxq(x, axis, fmt="e4m3"):
    dtype, down = {"e4m3": (ml_dtypes.float8_e4m3fn, 7), "e5m2": (ml_dtypes.float8_e5m2, 14)}[fmt]
    v = np.moveaxis(np.asarray(x, np.float32).astype(ml_dtypes.bfloat16).astype(np.float64), axis, -1)
    blocks = v.reshape(v.shape[:-1] + (-1, 32))
    amax = np.abs(blocks).max(-1, keepdims=True)
    byte = np.maximum(np.where(amax > 0, np.frexp(amax)[1] - 1 + 127, 0) - down, 1)
    scale = np.exp2(byte - 127.0)
    codes = (blocks / scale).astype(np.float32).astype(dtype).astype(np.float64)
    return np.moveaxis((codes * scale).reshape(v.shape), -1, axis)


WIDE = False


def mx_kscale(k):
    if not WIDE:
        return np.ones(k)
    levels = np.array([10, -10, 5, -5, 0])
    if k % 512:
        return np.exp2(np.random.permutation(np.resize(levels, k // 32))).repeat(32)
    a = np.empty((k // 512, 16))
    for p in range(k // 512):
        a[p, :8] = np.random.permutation(np.resize(levels, 8))
        for g in range(8):
            far = levels[np.abs(levels - a[p, g]) >= 10]
            a[p, g + 8] = far[np.random.randint(len(far))]
    return np.exp2(a.ravel()).repeat(32)


def f64(x):
    return np.asarray(x).astype(np.float64)


def striped(idx):
    return np.tile(idx.reshape(-1, 16).T, (8, 1)).astype(np.uint16)


def unstriped(offs):
    return offs[:16].T.reshape(-1).astype(np.int64)


def striped8(idx):
    return np.concatenate([x.reshape(-1, 16).T for x in idx]).astype(np.uint16)


def runs(offs, k):
    lists = np.stack([offs[16 * r : 16 * r + 16].T.reshape(-1) for r in range(8)]).astype(np.int64)
    return lists[np.arange(k) % 512 // 64]


def pack_weight(w):
    k, n = w.shape
    w = f64(np.asarray(w, np.float32).astype(ml_dtypes.bfloat16)).reshape(k // 32, 32, n)
    amax = np.abs(w).max(1)
    byte = np.clip(np.where(amax > 0, np.frexp(amax)[1] - 1 + 127 - 7, 1), 1, 254)
    scaled = (w * np.exp2(127.0 - byte)[:, None, :]).reshape(k, n).astype(np.float32)
    words = np.ascontiguousarray(scaled.reshape(k // 512, 128, 4, n).transpose(0, 1, 3, 2)).astype(ml_dtypes.float8_e4m3fn).view(np.uint8)
    return words, np.ascontiguousarray(byte.astype(np.uint8).reshape(k // 512, 16, n))


def unpack_weight(words, scales):
    g, p, n, _ = words.shape
    vals = np.ascontiguousarray(words).view(ml_dtypes.float8_e4m3fn).astype(np.float64) * np.repeat(np.exp2(scales.astype(np.float64) - 127.0), 8, axis=1)[..., None]
    return vals.transpose(0, 1, 3, 2).reshape(g * 512, n)


def relu(v):
    return np.maximum(v, 0.0)

def planes(y):
    n, m = y.shape
    v = y.astype(np.float32).astype(ml_dtypes.bfloat16).astype(np.float64).reshape(n // 32, 32, m)
    top = np.abs(v).max(1)
    byte = np.clip(np.where(top > 0, np.frexp(top)[1] - 1 + 127 - 7, 1), 1, 254)
    codes = (v * np.exp2(127.0 - byte)[:, None, :]).reshape(n, m).astype(np.float32).astype(ml_dtypes.float8_e4m3fn).view(np.uint8)
    words = codes.reshape(n // 512, 128, 4, m).transpose(0, 1, 3, 2)
    return np.ascontiguousarray(words), np.ascontiguousarray(byte.astype(np.uint8).reshape(n // 512, 16, m))


K, T, S, N, H, U = 512, 2048, 512, 512, 512, 1024


def setup_inputs():
    n = np.random.standard_normal
    s = mx_kscale(K)[:, None]
    u = mx_kscale(H)
    packed_xT = pack_weight(n((K, T)) * s)
    packed_w1 = pack_weight(n((K, H)) / np.sqrt(K) / s)
    packed_w2 = pack_weight(n((H, N)) / np.sqrt(2 * H) / u[:, None])
    packed_w3 = pack_weight(n((H, N)) / np.sqrt(2 * H) / u[:, None])
    return {
        "x_words": packed_xT[0],
        "x_scales": packed_xT[1],
        "w1_words": packed_w1[0],
        "w1_scales": packed_w1[1],
        "gn": (np.random.uniform(0.5, 1.5, (H, 1)) * u[:, None]).astype(np.float32),
        "gm": (np.random.uniform(0.5, 1.5, (H, 1)) * u[:, None]).astype(np.float32),
        "w2_words": packed_w2[0],
        "w2_scales": packed_w2[1],
        "w3_words": packed_w3[0],
        "w3_scales": packed_w3[1],
        "offs": striped(np.random.permutation(T)[:S]),
        "n1": striped8(np.stack([np.random.permutation(S) for _ in range(8)])),
        "n2": striped8(np.stack([np.random.permutation(S) for _ in range(8)])),
        "n3": striped8(np.stack([np.random.permutation(S) for _ in range(8)])),
        "n4": striped8(np.stack([np.random.permutation(S) for _ in range(8)])),
        "n5": striped8(np.stack([np.random.permutation(S) for _ in range(8)])),
        "n6": striped8(np.stack([np.random.permutation(U)[:S] for _ in range(8)])),
        "n7": striped8(np.stack([np.random.permutation(S) for _ in range(8)])),
    }


def reference(x_words, x_scales, w1_words, w1_scales, gn, gm, w2_words, w2_scales, w3_words, w3_scales, offs, n1, n2, n3, n4, n5, n6, n7):
    xq = unpack_weight(x_words, x_scales)[:, unstriped(offs)]
    y = unpack_weight(w1_words, w1_scales).T @ xq
    st = y + y[np.arange(H)[:, None], runs(n1, H)]
    z = f64(gn) * (st * (np.tanh(st[np.arange(H)[:, None], runs(n2, H)])))
    z2 = f64(gm) * (y + y[np.arange(H)[:, None], runs(n3, H)] - (np.maximum(y[np.arange(H)[:, None], runs(n4, H)], y[np.arange(H)[:, None], runs(n5, H)])))
    h = unpack_weight(w2_words, w2_scales).T @ mxq(z, 0, "e4m3") + unpack_weight(w3_words, w3_scales).T @ mxq(z2, 0, "e4m3")
    nw = h - (relu(h[np.arange(N)[:, None], runs(n7, N)]))
    out = np.zeros((N, U))
    out[np.arange(N)[:, None], runs(n6, N)] = nw
    return (out,) + planes(out)

@@ -1,0 +1,250 @@
+from contextlib import ExitStack
+
+import concourse.mybir as mybir
+
+K, T, S, N, H, U = 512, 2048, 512, 512, 512, 1024
+FLOPS = 3 * 2 * 512 * 512 * 512
+
+F32 = mybir.dt.float32
+BF16 = mybir.dt.bfloat16
+I32 = mybir.dt.int32
+U32 = mybir.dt.uint32
+U16 = mybir.dt.uint16
+U8 = mybir.dt.uint8
+FP8X4 = mybir.dt.float8_e4m3fn_x4
+ALU = mybir.AluOpType
+ACT = mybir.ActivationFunctionType
+
+P = 128
+PACK = 4
+HALF = U // 2
+
+
+def load_words(queue, tile, words):
+    queue.dma_start(out=tile[:].bitcast(I32), in_=words[0].rearrange("p c r -> p (c r)").bitcast(I32))
+
+
+def load_scales(queue, tile, first_row, scales):
+    for q in range(4):
+        row = 32 * q + first_row
+        queue.dma_start(out=tile[row : row + 4, :].bitcast(I32), in_=scales[0, 4 * q : 4 * q + 4, :].bitcast(I32))
+
+
+def deal(nc, dealt, raw):
+    nc.vector.tensor_copy(
+        out=dealt[:].rearrange("p (t m) -> p t m", t=PACK), in_=raw[:].rearrange("p (m t) -> p t m", t=PACK)
+    )
+
+
+def tile_picked_joinhopptrimpagez_none_po_kernel(
+    tc, x_words, x_scales, w1_words, w1_scales, gn, gm, w2_words, w2_scales, w3_words, w3_scales,
+    offs, n1, n2, n3, n4, n5, n6, n7, out_0, out_1, out_2,
+):
+    nc = tc.nc
+    with ExitStack() as ctx:
+        lists = ctx.enter_context(tc.tile_pool(name="lists", bufs=1))
+        keep = ctx.enter_context(tc.tile_pool(name="keep", bufs=1))
+        psum = ctx.enter_context(tc.psum_pool(name="psum", bufs=1))
+
+        def sb(name, shape, dtype):
+            return keep.tile(shape, dtype, name=name, align_bytes=64)
+
+        def load_list(name, src):
+            tile = lists.tile([P, S // 16], U16, name=name)
+            nc.sync.dma_start(tile[:], src)
+            return tile
+
+        xw = sb("xw", [P, T], U32)
+        xs = sb("xs", [P, T], U8)
+        w1w = sb("w1w", [P, H], I32)
+        w1s = sb("w1s", [P, H], U8)
+        w2w = sb("w2w", [P, N], I32)
+        w3w = sb("w3w", [P, N], I32)
+        w23s = sb("w23s", [P, N], U8)
+        nc.vector.memset(xs[:].bitcast(I32), 0)
+        nc.vector.memset(w1s[:].bitcast(I32), 0)
+        nc.gpsimd.memset(w23s[:].bitcast(I32), 0)
+
+        l_offs = load_list("l_offs", offs)
+        load_words(nc.sync, w1w, w1_words)
+        load_scales(nc.sync, xs, 0, x_scales)
+        load_words(nc.scalar, xw, x_words)
+        load_scales(nc.sync, w1s, 0, w1_scales)
+        l3 = load_list("l3", n3)
+        l1 = load_list("l1", n1)
+        l4 = load_list("l4", n4)
+        l5 = load_list("l5", n5)
+        load_words(nc.sync, w2w, w2_words)
+        load_words(nc.sync, w3w, w3_words)
+        l2 = load_list("l2", n2)
+        gn_sb = sb("gn_sb", [P, PACK], F32)
+        gm_sb = sb("gm_sb", [P, PACK], F32)
+        nc.sync.dma_start(out=gn_sb[:], in_=gn.rearrange("(p t) o -> p (t o)", t=PACK))
+        nc.sync.dma_start(out=gm_sb[:], in_=gm.rearrange("(p t) o -> p (t o)", t=PACK))
+        load_scales(nc.sync, w23s, 0, w2_scales)
+        load_scales(nc.sync, w23s, 4, w3_scales)
+        l7 = load_list("l7", n7)
+        l6 = load_list("l6", n6)
+
+        page = [sb("page%d" % t, [P, U], F32) for t in range(PACK)]
+        y_slot = [sb("y_slot%d" % t, [P, 2 * S], F32) for t in range(PACK + 1)]
+        h_slot = [sb("h_slot%d" % t, [P, 2 * S], F32) for t in range(PACK + 1)]
+        st_win = [sb("st_win%d" % t, [P, 2 * S], F32) for t in range(PACK)]
+        minus_one = sb("minus_one", [P, S], F32)
+        nc.gpsimd.memset(y_slot[0][:, S:], 0.0)
+        nc.gpsimd.memset(h_slot[0][:, S:], 0.0)
+        nc.gpsimd.memset(minus_one[:], -1.0)
+        for t in range(PACK):
+            nc.vector.memset(page[t][:], 0.0)
+
+        gn_twice = sb("gn_twice", [P, PACK], F32)
+        gn_neg = sb("gn_neg", [P, PACK], F32)
+        gm_neg = sb("gm_neg", [P, PACK], F32)
+        nc.gpsimd.tensor_scalar(gn_twice[:], gn_sb[:], 2.0, 0.0, ALU.mult, ALU.add)
+        nc.gpsimd.tensor_scalar(gn_neg[:], gn_sb[:], -1.0, 0.0, ALU.mult, ALU.add)
+        nc.gpsimd.tensor_scalar(gm_neg[:], gm_sb[:], -1.0, 0.0, ALU.mult, ALU.add)
+
+        xs_picked = sb("xs_picked", [P, S], U8)
+        xw_picked = sb("xw_picked", [P, S], U32)
+        w1w_dealt = sb("w1w_dealt", [P, H], I32)
+        w1s_dealt = sb("w1s_dealt", [P, H], U8)
+        nc.vector.tensor_copy(xs_picked[:], xs[:].indirect(l_offs[:]))
+        deal(nc, w1w_dealt, w1w)
+        deal(nc, w1s_dealt, w1s)
+        nc.vector.tensor_copy(xw_picked[:], xw[:].indirect(l_offs[:]))
+
+        y_bank = [psum.tile([P, S], F32, name="y_bank%d" % t) for t in range(PACK)]
+        for t in range(PACK):
+            cols = slice(t * P, (t + 1) * P)
+            nc.tensor.matmul_mx(
+                out=y_bank[t][:], lhsT=w1w_dealt[:, cols].bitcast(FP8X4), lhsT_scale=w1s_dealt[:, cols],
+                rhs=xw_picked[:].bitcast(FP8X4), rhs_scale=xs_picked[:], start=True, stop=True,
+            )
+
+        w2w_dealt = sb("w2w_dealt", [P, N], I32)
+        w3w_dealt = sb("w3w_dealt", [P, N], I32)
+        w23s_dealt = sb("w23s_dealt", [P, N], U8)
+        deal(nc, w2w_dealt, w2w)
+        deal(nc, w3w_dealt, w3w)
+        deal(nc, w23s_dealt, w23s)
+
+        st4 = sb("st4", [P, PACK, S], F32)
+        sig4 = sb("sig4", [P, PACK, S], F32)
+        tanh4 = sb("tanh4", [P, PACK, S], F32)
+        a4 = sb("a4", [P, PACK, S], F32)
+        b4 = sb("b4", [P, PACK, S], F32)
+        m4 = sb("m4", [P, PACK, S], F32)
+        z_bf = sb("z_bf", [P, PACK * S], BF16)
+        z2_bf = sb("z2_bf", [P, PACK * S], BF16)
+
+        def leave_y(t):
+            nc.scalar.copy(y_slot[t][:, :S], y_bank[t][:])
+            nc.scalar.copy(y_slot[t + 1][:, S:], y_bank[t][:])
+
+        def first_sum(t):
+            nc.vector.tensor_tensor(st_win[t][:, S:], y_slot[t][:].indirect(l3[:]), y_slot[t + 1][:, S:], ALU.add)
+
+        def larger(t):
+            nc.vector.tensor_tensor(m4[:, t, :], a4[:, t, :], b4[:, t, :], ALU.max)
+
+        def round_z2(t):
+            nc.scalar.activation(
+                z2_bf[:].rearrange("p (j t) -> p t j", t=PACK)[:, t, :], m4[:, t, :], ACT.Copy,
+                scale=gm_neg[:, t : t + 1],
+            )
+
+        def product_z(c0, c1):
+            nc.vector.tensor_tensor(
+                z_bf[:].rearrange("p (c i t) -> p c t i", i=2, t=PACK)[:, c0:c1],
+                tanh4[:].rearrange("p t (c i) -> p c t i", i=2)[:, c0:c1],
+                st4[:].rearrange("p t (c i) -> p c t i", i=2)[:, c0:c1],
+                ALU.mult,
+            )
+
+        leave_y(0)
+        first_sum(0)
+        for t in range(PACK):
+            window = y_slot[t][:]
+            u = st_win[t][:, S:]
+            if t + 1 < PACK:
+                leave_y(t + 1)
+            nc.vector.tensor_tensor(st_win[t][:, :S], window.indirect(l1[:]), y_slot[t + 1][:, S:], ALU.add)
+            nc.scalar.activation(sig4[:, t, :], st_win[t][:].indirect(l2[:]), ACT.Sigmoid, scale=2.0)
+            nc.scalar.activation(
+                tanh4[:, t, :], sig4[:, t, :], ACT.Identity, scale=gn_twice[:, t : t + 1], bias=gn_neg[:, t : t + 1]
+            )
+            nc.scalar.copy(st4[:, t, :], st_win[t][:, :S])
+            nc.vector.tensor_tensor(a4[:, t, :], window.indirect(l4[:]), u, ALU.subtract)
+            nc.vector.tensor_tensor(b4[:, t, :], window.indirect(l5[:]), u, ALU.subtract)
+            if t + 1 < PACK:
+                first_sum(t + 1)
+            else:
+                product_z(0, S // 4)
+            larger(t)
+            round_z2(t)
+        product_z(S // 4, S // 2)
+
+        z_codes = sb("z_codes", [P, S], U32)
+        z_scales = sb("z_scales", [P, S], U8)
+        z2_codes = sb("z2_codes", [P, S], U32)
+        z2_scales = sb("z2_scales", [P, S], U8)
+        nc.vector.quantize_mx(out=z_codes[:].bitcast(FP8X4), scales=z_scales[:], in_=z_bf[:])
+        nc.vector.quantize_mx(out=z2_codes[:].bitcast(FP8X4), scales=z2_scales[:], in_=z2_bf[:])
+
+        h_bank = [psum.tile([P, S], F32, name="h_bank%d" % t) for t in range(PACK)]
+        for t in range(PACK):
+            cols = slice(t * P, (t + 1) * P)
+            nc.tensor.matmul_mx(
+                out=h_bank[t][:], lhsT=w2w_dealt[:, cols].bitcast(FP8X4), lhsT_scale=w23s_dealt[:, cols],
+                rhs=z_codes[:].bitcast(FP8X4), rhs_scale=z_scales[:], start=True, stop=False,
+            )
+        for t in range(PACK):
+            cols = slice(t * P, (t + 1) * P)
+            nc.tensor.matmul_mx(
+                out=h_bank[t][:], lhsT=w3w_dealt[:, cols].bitcast(FP8X4), lhsT_scale=w23s_dealt[4:, cols],
+                rhs=z2_codes[:].bitcast(FP8X4), rhs_scale=z2_scales[:], start=False, stop=True,
+            )
+
+        nw_neg = sb("nw_neg", [P, PACK, S], F32)
+        page_bf = sb("page_bf", [P, PACK * U], BF16)
+        page_codes = sb("page_codes", [P, U], U32)
+        page_scales = sb("page_scales", [P, U], U8)
+        rows = out_0.rearrange("(p t) c -> p t c", t=PACK)
+        planes = page_bf[:].rearrange("p (c t) -> p t c", t=PACK)
+        by_column = page_bf[:].rearrange("p (c t) -> p c t", t=PACK)
+
+        for t in range(PACK):
+            nc.scalar.activation(h_slot[t][:, :S], h_bank[t][:], ACT.Relu)
+            nc.scalar.copy(h_slot[t + 1][:, S:], h_bank[t][:])
+
+        def look_up_h(t):
+            nc.vector.tensor_tensor(nw_neg[:, t, :], h_slot[t][:].indirect(l7[:]), h_slot[t + 1][:, S:], ALU.subtract)
+
+        for t in range(PACK):
+            if t != 2:
+                look_up_h(t)
+            if t == 1:
+                look_up_h(2)
+            nc.vector.tensor_tensor(page[t][:].indirect(l6[:]), nw_neg[:, t, :], minus_one[:], ALU.mult)
+            nc.sync.dma_start(out=rows[:, t, :], in_=page[t][:])
+            if t < 2:
+                nc.scalar.copy(planes[:, t, :], page[t][:])
+            elif t == 2:
+                nc.scalar.copy(by_column[:, :, 2:], page[t][:].unsqueeze(2).to_broadcast([P, U, 2]))
+            else:
+                nc.vector.tensor_copy(planes[:, t, :HALF], page[t][:, :HALF])
+                nc.scalar.copy(planes[:, t, HALF:], page[t][:, HALF:])
+
+        words = out_1[0].rearrange("p c r -> p (c r)").bitcast(I32)
+        for half in range(2):
+            cols = slice(half * HALF, (half + 1) * HALF)
+            nc.vector.quantize_mx(
+                out=page_codes[:, cols].bitcast(FP8X4), scales=page_scales[:, cols],
+                in_=page_bf[:, PACK * cols.start : PACK * cols.stop],
+            )
+            nc.sync.dma_start(out=words[:, cols], in_=page_codes[:, cols].bitcast(I32))
+        for q in range(4):
+            queue = nc.scalar if q % 2 == 0 else nc.sync
+            queue.dma_start(
+                out=out_2[0, 4 * q : 4 * q + 4, :].bitcast(I32), in_=page_scales[32 * q : 32 * q + 4, :].bitcast(I32)
+            )

@@ -21,18 +21,18 @@ HALF = U // 2
 
 
 def load_words(queue, tile, words):
-    queue.dma_start(out=tile[:].bitcast(I32), in_=words[0].rearrange("p c r -> p (c r)").bitcast(I32))
+    queue.dma_start(out=tile.bitcast(I32), in_=words[0].rearrange("p c r -> p (c r)").bitcast(I32))
 
 
-def load_scales(queue, tile, first_row, scales):
+def load_scales(queues, tile, first_row, scales):
     for q in range(4):
         row = 32 * q + first_row
-        queue.dma_start(out=tile[row : row + 4, :].bitcast(I32), in_=scales[0, 4 * q : 4 * q + 4, :].bitcast(I32))
+        queues[q].dma_start(out=tile[row : row + 4, :].bitcast(I32), in_=scales[0, 4 * q : 4 * q + 4, :].bitcast(I32))
 
 
 def deal(nc, dealt, raw):
     nc.vector.tensor_copy(
-        out=dealt[:].rearrange("p (t m) -> p t m", t=PACK), in_=raw[:].rearrange("p (m t) -> p t m", t=PACK)
+        out=dealt.rearrange("p (t m) -> p t m", t=PACK), in_=raw.rearrange("p (m t) -> p t m", t=PACK)
     )
 
 
@@ -46,8 +46,8 @@ def tile_picked_joinhopptrimpagez_none_po_kernel(
         keep = ctx.enter_context(tc.tile_pool(name="keep", bufs=1))
         psum = ctx.enter_context(tc.psum_pool(name="psum", bufs=1))
 
-        def sb(name, shape, dtype):
-            return keep.tile(shape, dtype, name=name, align_bytes=64)
+        def sb(name, shape, dtype, tag=None):
+            return keep.tile(shape, dtype, name=name, tag=tag or name, align_bytes=64)
 
         def load_list(name, src):
             tile = lists.tile([P, S // 16], U16, name=name)
@@ -56,46 +56,34 @@ def tile_picked_joinhopptrimpagez_none_po_kernel(
 
         xw = sb("xw", [P, T], U32)
         xs = sb("xs", [P, T], U8)
-        w1w = sb("w1w", [P, H], I32)
+        w1w = keep.tile([P, H], I32, name="w1w", tag="w_raw", align_bytes=64)
         w1s = sb("w1s", [P, H], U8)
-        w2w = sb("w2w", [P, N], I32)
-        w3w = sb("w3w", [P, N], I32)
-        w23s = sb("w23s", [P, N], U8)
         nc.vector.memset(xs[:].bitcast(I32), 0)
         nc.vector.memset(w1s[:].bitcast(I32), 0)
-        nc.gpsimd.memset(w23s[:].bitcast(I32), 0)
-
-        l_offs = load_list("l_offs", offs)
-        load_words(nc.sync, w1w, w1_words)
-        load_scales(nc.sync, xs, 0, x_scales)
-        load_words(nc.scalar, xw, x_words)
-        load_scales(nc.sync, w1s, 0, w1_scales)
-        l3 = load_list("l3", n3)
-        l1 = load_list("l1", n1)
-        l4 = load_list("l4", n4)
-        l5 = load_list("l5", n5)
-        load_words(nc.sync, w2w, w2_words)
-        load_words(nc.sync, w3w, w3_words)
-        l2 = load_list("l2", n2)
         gn_sb = sb("gn_sb", [P, PACK], F32)
         gm_sb = sb("gm_sb", [P, PACK], F32)
+
+        l_offs = load_list("l_offs", offs)
+        l1 = load_list("l1", n1)
+        load_words(nc.sync, w1w[:], w1_words)
+        load_words(nc.sync, xw[:], x_words)
+        load_scales([nc.scalar] * 4, xs, 0, x_scales)
+        load_scales([nc.gpsimd, nc.scalar, nc.scalar, nc.scalar], w1s, 0, w1_scales)
+        l3 = load_list("l3", n3)
+        l4 = load_list("l4", n4)
+        l5 = load_list("l5", n5)
+        l2 = load_list("l2", n2)
         nc.sync.dma_start(out=gn_sb[:], in_=gn.rearrange("(p t) o -> p (t o)", t=PACK))
         nc.sync.dma_start(out=gm_sb[:], in_=gm.rearrange("(p t) o -> p (t o)", t=PACK))
-        load_scales(nc.sync, w23s, 0, w2_scales)
-        load_scales(nc.sync, w23s, 4, w3_scales)
         l7 = load_list("l7", n7)
         l6 = load_list("l6", n6)
 
-        page = [sb("page%d" % t, [P, U], F32) for t in range(PACK)]
         y_slot = [sb("y_slot%d" % t, [P, 2 * S], F32) for t in range(PACK + 1)]
-        h_slot = [sb("h_slot%d" % t, [P, 2 * S], F32) for t in range(PACK + 1)]
-        st_win = [sb("st_win%d" % t, [P, 2 * S], F32) for t in range(PACK)]
-        minus_one = sb("minus_one", [P, S], F32)
-        nc.gpsimd.memset(y_slot[0][:, S:], 0.0)
-        nc.gpsimd.memset(h_slot[0][:, S:], 0.0)
-        nc.gpsimd.memset(minus_one[:], -1.0)
-        for t in range(PACK):
-            nc.vector.memset(page[t][:], 0.0)
+        st_slot = [sb("st_slot%d" % t, [P, 2 * S], F32) for t in range(PACK + 1)]
+        nc.vector.memset(y_slot[0][:, S:], 0.0)
+        nc.vector.memset(st_slot[0][:, S:], 0.0)
+        warm = sb("warm", [P, 16], F32)
+        nc.scalar.activation(warm[:, 0:1], st_slot[0][:, S : S + 1], ACT.Sigmoid)
 
         gn_twice = sb("gn_twice", [P, PACK], F32)
         gn_neg = sb("gn_neg", [P, PACK], F32)
@@ -108,25 +96,43 @@ def tile_picked_joinhopptrimpagez_none_po_kernel(
         xw_picked = sb("xw_picked", [P, S], U32)
         w1w_dealt = sb("w1w_dealt", [P, H], I32)
         w1s_dealt = sb("w1s_dealt", [P, H], U8)
-        nc.vector.tensor_copy(xs_picked[:], xs[:].indirect(l_offs[:]))
-        deal(nc, w1w_dealt, w1w)
-        deal(nc, w1s_dealt, w1s)
-        nc.vector.tensor_copy(xw_picked[:], xw[:].indirect(l_offs[:]))
+        deal(nc, w1w_dealt[:], w1w[:])
+        halves = [slice(0, S // 2), slice(S // 2, S)]
+        list_halves = [slice(0, S // 32), slice(S // 32, S // 16)]
+        for k in range(2):
+            nc.vector.tensor_copy(xs_picked[:, halves[k]], xs[:].indirect(l_offs[:, list_halves[k]]))
+        deal(nc, w1s_dealt[:], w1s[:])
+        for k in range(2):
+            nc.vector.tensor_copy(xw_picked[:, halves[k]], xw[:].indirect(l_offs[:, list_halves[k]]))
 
-        y_bank = [psum.tile([P, S], F32, name="y_bank%d" % t) for t in range(PACK)]
+        def banks(name):
+            return [
+                [psum.tile([P, S // 2], F32, name="%s%d_%d" % (name, t, k), tag="bank%d_%d" % (t, k)) for k in range(2)]
+                for t in range(PACK)
+            ]
+
+        y_bank = banks("y")
         for t in range(PACK):
             cols = slice(t * P, (t + 1) * P)
-            nc.tensor.matmul_mx(
-                out=y_bank[t][:], lhsT=w1w_dealt[:, cols].bitcast(FP8X4), lhsT_scale=w1s_dealt[:, cols],
-                rhs=xw_picked[:].bitcast(FP8X4), rhs_scale=xs_picked[:], start=True, stop=True,
-            )
+            for k in range(2):
+                nc.tensor.matmul_mx(
+                    out=y_bank[t][k][:], lhsT=w1w_dealt[:, cols].bitcast(FP8X4), lhsT_scale=w1s_dealt[:, cols],
+                    rhs=xw_picked[:, halves[k]].bitcast(FP8X4), rhs_scale=xs_picked[:, halves[k]],
+                    start=True, stop=True,
+                )
 
-        w2w_dealt = sb("w2w_dealt", [P, N], I32)
-        w3w_dealt = sb("w3w_dealt", [P, N], I32)
+        w23w_dealt = sb("w23w_dealt", [P, 2 * N], I32, tag="xw")
+        w2w_dealt = w23w_dealt[:, :N]
+        w3w_dealt = w23w_dealt[:, N:]
         w23s_dealt = sb("w23s_dealt", [P, N], U8)
-        deal(nc, w2w_dealt, w2w)
-        deal(nc, w3w_dealt, w3w)
-        deal(nc, w23s_dealt, w23s)
+        w23w = keep.tile([P, 2 * N], I32, name="w23w", tag="w_raw", align_bytes=64)
+        load_words(nc.sync, w23w[:, :N], w2_words)
+        load_words(nc.sync, w23w[:, N:], w3_words)
+        load_scales([nc.sync] * 4, w1s, 4, w2_scales)
+        load_scales([nc.sync] * 4, w1s, 8, w3_scales)
+        deal(nc, w2w_dealt, w23w[:, :N])
+        deal(nc, w3w_dealt, w23w[:, N:])
+        deal(nc, w23s_dealt[:], w1s[:])
 
         st4 = sb("st4", [P, PACK, S], F32)
         sig4 = sb("sig4", [P, PACK, S], F32)
@@ -138,20 +144,30 @@ def tile_picked_joinhopptrimpagez_none_po_kernel(
         z2_bf = sb("z2_bf", [P, PACK * S], BF16)
 
         def leave_y(t):
-            nc.scalar.copy(y_slot[t][:, :S], y_bank[t][:])
-            nc.scalar.copy(y_slot[t + 1][:, S:], y_bank[t][:])
+            for k in range(2):
+                nc.scalar.copy(y_slot[t][:, :S][:, halves[k]], y_bank[t][k][:])
+                nc.scalar.copy(y_slot[t + 1][:, S:][:, halves[k]], y_bank[t][k][:])
 
         def first_sum(t):
-            nc.vector.tensor_tensor(st_win[t][:, S:], y_slot[t][:].indirect(l3[:]), y_slot[t + 1][:, S:], ALU.add)
+            nc.vector.tensor_tensor(st_slot[t + 1][:, S:], y_slot[t][:].indirect(l3[:]), y_slot[t + 1][:, S:], ALU.add)
+
+        def gated_sum(t):
+            nc.vector.tensor_tensor(st_slot[t][:, :S], y_slot[t][:].indirect(l1[:]), y_slot[t + 1][:, S:], ALU.add)
+            nc.sync.dma_start(out=st4[:, t, :], in_=st_slot[t][:, :S])
+            nc.scalar.activation(sig4[:, t, :], st_slot[t][:].indirect(l2[:]), ACT.Sigmoid, scale=2.0)
+            nc.scalar.activation(
+                tanh4[:, t, :], sig4[:, t, :], ACT.Identity, scale=gn_twice[:, t : t + 1], bias=gn_neg[:, t : t + 1]
+            )
 
         def larger(t):
             nc.vector.tensor_tensor(m4[:, t, :], a4[:, t, :], b4[:, t, :], ALU.max)
 
         def round_z2(t):
-            nc.scalar.activation(
-                z2_bf[:].rearrange("p (j t) -> p t j", t=PACK)[:, t, :], m4[:, t, :], ACT.Copy,
-                scale=gm_neg[:, t : t + 1],
-            )
+            plane = z2_bf[:].rearrange("p (j t) -> p t j", t=PACK)[:, t, :]
+            for k in range(2):
+                nc.scalar.activation(
+                    plane[:, halves[k]], m4[:, t, halves[k]], ACT.Copy, scale=gm_neg[:, t : t + 1]
+                )
 
         def product_z(c0, c1):
             nc.vector.tensor_tensor(
@@ -161,19 +177,15 @@ def tile_picked_joinhopptrimpagez_none_po_kernel(
                 ALU.mult,
             )
 
-        leave_y(0)
+        for t in range(PACK):
+            leave_y(t)
+        gated_sum(0)
         first_sum(0)
         for t in range(PACK):
             window = y_slot[t][:]
-            u = st_win[t][:, S:]
+            u = st_slot[t + 1][:, S:]
             if t + 1 < PACK:
-                leave_y(t + 1)
-            nc.vector.tensor_tensor(st_win[t][:, :S], window.indirect(l1[:]), y_slot[t + 1][:, S:], ALU.add)
-            nc.scalar.activation(sig4[:, t, :], st_win[t][:].indirect(l2[:]), ACT.Sigmoid, scale=2.0)
-            nc.scalar.activation(
-                tanh4[:, t, :], sig4[:, t, :], ACT.Identity, scale=gn_twice[:, t : t + 1], bias=gn_neg[:, t : t + 1]
-            )
-            nc.scalar.copy(st4[:, t, :], st_win[t][:, :S])
+                gated_sum(t + 1)
             nc.vector.tensor_tensor(a4[:, t, :], window.indirect(l4[:]), u, ALU.subtract)
             nc.vector.tensor_tensor(b4[:, t, :], window.indirect(l5[:]), u, ALU.subtract)
             if t + 1 < PACK:
@@ -184,26 +196,42 @@ def tile_picked_joinhopptrimpagez_none_po_kernel(
             round_z2(t)
         product_z(S // 4, S // 2)
 
+        page_tags = ["xw_picked", "xs", "w_raw", "w1s"]
+        page = [sb("page%d" % t, [P, U], F32, tag=page_tags[t]) for t in range(PACK)]
+        h_slot = [sb("h_slot%d" % t, [P, 2 * S], F32, tag="y_slot%d" % t) for t in range(PACK + 1)]
+        minus_one = sb("minus_one", [P, S], F32, tag="w1w_dealt")
+        nc.gpsimd.memset(h_slot[0][:, S:], 0.0)
+        nc.gpsimd.memset(minus_one[:], -1.0)
+        for t in range(PACK):
+            nc.gpsimd.memset(page[t][:], 0.0)
+
         z_codes = sb("z_codes", [P, S], U32)
         z_scales = sb("z_scales", [P, S], U8)
         z2_codes = sb("z2_codes", [P, S], U32)
         z2_scales = sb("z2_scales", [P, S], U8)
-        nc.vector.quantize_mx(out=z_codes[:].bitcast(FP8X4), scales=z_scales[:], in_=z_bf[:])
-        nc.vector.quantize_mx(out=z2_codes[:].bitcast(FP8X4), scales=z2_scales[:], in_=z2_bf[:])
+        for k in range(2):
+            wide = slice(PACK * halves[k].start, PACK * halves[k].stop)
+            nc.vector.quantize_mx(
+                out=z_codes[:, halves[k]].bitcast(FP8X4), scales=z_scales[:, halves[k]], in_=z_bf[:, wide]
+            )
+            nc.vector.quantize_mx(
+                out=z2_codes[:, halves[k]].bitcast(FP8X4), scales=z2_scales[:, halves[k]], in_=z2_bf[:, wide]
+            )
 
-        h_bank = [psum.tile([P, S], F32, name="h_bank%d" % t) for t in range(PACK)]
+        h_bank = banks("h")
         for t in range(PACK):
             cols = slice(t * P, (t + 1) * P)
-            nc.tensor.matmul_mx(
-                out=h_bank[t][:], lhsT=w2w_dealt[:, cols].bitcast(FP8X4), lhsT_scale=w23s_dealt[:, cols],
-                rhs=z_codes[:].bitcast(FP8X4), rhs_scale=z_scales[:], start=True, stop=False,
-            )
-        for t in range(PACK):
-            cols = slice(t * P, (t + 1) * P)
-            nc.tensor.matmul_mx(
-                out=h_bank[t][:], lhsT=w3w_dealt[:, cols].bitcast(FP8X4), lhsT_scale=w23s_dealt[4:, cols],
-                rhs=z2_codes[:].bitcast(FP8X4), rhs_scale=z2_scales[:], start=False, stop=True,
-            )
+            for k in range(2):
+                nc.tensor.matmul_mx(
+                    out=h_bank[t][k][:], lhsT=w2w_dealt[:, cols].bitcast(FP8X4), lhsT_scale=w23s_dealt[4:, cols],
+                    rhs=z_codes[:, halves[k]].bitcast(FP8X4), rhs_scale=z_scales[:, halves[k]],
+                    start=True, stop=False,
+                )
+                nc.tensor.matmul_mx(
+                    out=h_bank[t][k][:], lhsT=w3w_dealt[:, cols].bitcast(FP8X4), lhsT_scale=w23s_dealt[8:, cols],
+                    rhs=z2_codes[:, halves[k]].bitcast(FP8X4), rhs_scale=z2_scales[:, halves[k]],
+                    start=False, stop=True,
+                )
 
         nw_neg = sb("nw_neg", [P, PACK, S], F32)
         page_bf = sb("page_bf", [P, PACK * U], BF16)
@@ -214,8 +242,11 @@ def tile_picked_joinhopptrimpagez_none_po_kernel(
         by_column = page_bf[:].rearrange("p (c t) -> p c t", t=PACK)
 
         for t in range(PACK):
-            nc.scalar.activation(h_slot[t][:, :S], h_bank[t][:], ACT.Relu)
-            nc.scalar.copy(h_slot[t + 1][:, S:], h_bank[t][:])
+            for k in range(2):
+                nc.scalar.activation(h_slot[t][:, :S][:, halves[k]], h_bank[t][k][:], ACT.Relu)
+                nc.scalar.copy(h_slot[t + 1][:, S:][:, halves[k]], h_bank[t][k][:])
+
+        pieces = [slice(0, HALF), slice(HALF, HALF + U // 4), slice(HALF + U // 4, U)]
 
         def look_up_h(t):
             nc.vector.tensor_tensor(nw_neg[:, t, :], h_slot[t][:].indirect(l7[:]), h_slot[t + 1][:, S:], ALU.subtract)
@@ -233,11 +264,11 @@ def tile_picked_joinhopptrimpagez_none_po_kernel(
                 nc.scalar.copy(by_column[:, :, 2:], page[t][:].unsqueeze(2).to_broadcast([P, U, 2]))
             else:
                 nc.vector.tensor_copy(planes[:, t, :HALF], page[t][:, :HALF])
-                nc.scalar.copy(planes[:, t, HALF:], page[t][:, HALF:])
+                for cols in pieces[1:]:
+                    nc.scalar.copy(planes[:, t, cols], page[t][:, cols])
 
         words = out_1[0].rearrange("p c r -> p (c r)").bitcast(I32)
-        for half in range(2):
-            cols = slice(half * HALF, (half + 1) * HALF)
+        for cols in pieces:
             nc.vector.quantize_mx(
                 out=page_codes[:, cols].bitcast(FP8X4), scales=page_scales[:, cols],
                 in_=page_bf[:, PACK * cols.start : PACK * cols.stop],

@@ -2,7 +2,7 @@ from contextlib import ExitStack
 
 import concourse.mybir as mybir
 
-K, T, S, N, H, U = 512, 2048, 512, 512, 512, 1024
+T, S, N, H, U = 2048, 512, 512, 512, 1024
 FLOPS = 3 * 2 * 512 * 512 * 512
 
 F32 = mybir.dt.float32
@@ -16,23 +16,29 @@ ALU = mybir.AluOpType
 ACT = mybir.ActivationFunctionType
 
 P = 128
-PACK = 4
-HALF = U // 2
+PLANES = 4
+QUADRANTS = 4
+W1_ROW, W2_ROW, W3_ROW = 0, 4, 8
+
+HALVES = [slice(0, S // 2), slice(S // 2, S)]
+LIST_HALVES = [slice(0, S // 32), slice(S // 32, S // 16)]
+
+PIECES = [slice(0, U // 2), slice(U // 2, 3 * U // 4), slice(3 * U // 4, U)]
 
 
-def load_words(queue, tile, words):
-    queue.dma_start(out=tile.bitcast(I32), in_=words[0].rearrange("p c r -> p (c r)").bitcast(I32))
+def load_words(nc, words_sb, words):
+    nc.sync.dma_start(out=words_sb.bitcast(I32), in_=words[0].rearrange("p c r -> p (c r)").bitcast(I32))
 
 
-def load_scales(queues, tile, first_row, scales):
-    for q in range(4):
+def load_scales(nc, tile, first_row, scales):
+    for q in range(QUADRANTS):
         row = 32 * q + first_row
-        queues[q].dma_start(out=tile[row : row + 4, :].bitcast(I32), in_=scales[0, 4 * q : 4 * q + 4, :].bitcast(I32))
+        nc.sync.dma_start(out=tile[row : row + 4, :].bitcast(I32), in_=scales[0, 4 * q : 4 * q + 4, :].bitcast(I32))
 
 
 def deal(nc, dealt, raw):
     nc.vector.tensor_copy(
-        out=dealt.rearrange("p (t m) -> p t m", t=PACK), in_=raw.rearrange("p (m t) -> p t m", t=PACK)
+        out=dealt.rearrange("p (t m) -> p t m", t=PLANES), in_=raw.rearrange("p (m t) -> p t m", t=PLANES)
     )
 
 
@@ -54,70 +60,71 @@ def tile_picked_joinhopptrimpagez_none_po_kernel(
             nc.sync.dma_start(tile[:], src)
             return tile
 
+        def banks(name):
+            return [
+                [psum.tile([P, S // 2], F32, name="%s%d_%d" % (name, t, k), tag="bank%d_%d" % (t, k)) for k in range(2)]
+                for t in range(PLANES)
+            ]
+
         xw = sb("xw", [P, T], U32)
         xs = sb("xs", [P, T], U8)
-        w1w = keep.tile([P, H], I32, name="w1w", tag="w_raw", align_bytes=64)
-        w1s = sb("w1s", [P, H], U8)
+        w1w = sb("w1w", [P, H], I32, tag="w_raw")
+        ws = sb("ws", [P, H], U8)
         nc.vector.memset(xs[:].bitcast(I32), 0)
-        nc.vector.memset(w1s[:].bitcast(I32), 0)
-        gn_sb = sb("gn_sb", [P, PACK], F32)
-        gm_sb = sb("gm_sb", [P, PACK], F32)
+        nc.vector.memset(ws[:].bitcast(I32), 0)
+        gn_sb = sb("gn_sb", [P, PLANES], F32)
+        gm_sb = sb("gm_sb", [P, PLANES], F32)
 
         l_offs = load_list("l_offs", offs)
         l1 = load_list("l1", n1)
-        load_words(nc.sync, w1w[:], w1_words)
-        load_words(nc.sync, xw[:], x_words)
-        load_scales([nc.scalar] * 4, xs, 0, x_scales)
-        load_scales([nc.gpsimd, nc.scalar, nc.scalar, nc.scalar], w1s, 0, w1_scales)
+        load_words(nc, w1w[:], w1_words)
+        load_scales(nc, xs, 0, x_scales)
         l3 = load_list("l3", n3)
         l4 = load_list("l4", n4)
+        load_words(nc, xw[:], x_words)
+        load_scales(nc, ws, W1_ROW, w1_scales)
         l5 = load_list("l5", n5)
         l2 = load_list("l2", n2)
-        nc.sync.dma_start(out=gn_sb[:], in_=gn.rearrange("(p t) o -> p (t o)", t=PACK))
-        nc.sync.dma_start(out=gm_sb[:], in_=gm.rearrange("(p t) o -> p (t o)", t=PACK))
+        nc.sync.dma_start(out=gn_sb[:], in_=gn.rearrange("(p t) o -> p (t o)", t=PLANES))
+        nc.sync.dma_start(out=gm_sb[:], in_=gm.rearrange("(p t) o -> p (t o)", t=PLANES))
         l7 = load_list("l7", n7)
         l6 = load_list("l6", n6)
 
-        y_slot = [sb("y_slot%d" % t, [P, 2 * S], F32) for t in range(PACK + 1)]
-        st_slot = [sb("st_slot%d" % t, [P, 2 * S], F32) for t in range(PACK + 1)]
-        nc.vector.memset(y_slot[0][:, S:], 0.0)
-        nc.vector.memset(st_slot[0][:, S:], 0.0)
-        warm = sb("warm", [P, 16], F32)
-        nc.scalar.activation(warm[:, 0:1], st_slot[0][:, S : S + 1], ACT.Sigmoid)
+        y_tile = [sb("y_tile%d" % t, [P, 2 * S], F32) for t in range(PLANES + 1)]
+        st_tile = [sb("st_tile%d" % t, [P, 2 * S], F32) for t in range(PLANES + 1)]
+        minus_one = y_tile[0][:, S:]
+        nc.vector.memset(minus_one, -1.0)
+        nc.vector.memset(st_tile[0][:, S:], 0.0)
 
-        gn_twice = sb("gn_twice", [P, PACK], F32)
-        gn_neg = sb("gn_neg", [P, PACK], F32)
-        gm_neg = sb("gm_neg", [P, PACK], F32)
-        nc.gpsimd.tensor_scalar(gn_twice[:], gn_sb[:], 2.0, 0.0, ALU.mult, ALU.add)
-        nc.gpsimd.tensor_scalar(gn_neg[:], gn_sb[:], -1.0, 0.0, ALU.mult, ALU.add)
-        nc.gpsimd.tensor_scalar(gm_neg[:], gm_sb[:], -1.0, 0.0, ALU.mult, ALU.add)
+        early_pages = [sb("page%d" % t, [P, U], F32) for t in (2, 3)]
+        for tile in early_pages:
+            nc.vector.memset(tile[:], 0.0)
+
+        gn_twice = sb("gn_twice", [P, PLANES], F32)
+        gn_neg = sb("gn_neg", [P, PLANES], F32)
+        gm_neg = sb("gm_neg", [P, PLANES], F32)
+        nc.scalar.mul(gn_twice[:], gn_sb[:], 2.0)
+        nc.scalar.mul(gn_neg[:], gn_sb[:], -1.0)
+        nc.scalar.mul(gm_neg[:], gm_sb[:], -1.0)
 
         xs_picked = sb("xs_picked", [P, S], U8)
         xw_picked = sb("xw_picked", [P, S], U32)
         w1w_dealt = sb("w1w_dealt", [P, H], I32)
         w1s_dealt = sb("w1s_dealt", [P, H], U8)
         deal(nc, w1w_dealt[:], w1w[:])
-        halves = [slice(0, S // 2), slice(S // 2, S)]
-        list_halves = [slice(0, S // 32), slice(S // 32, S // 16)]
         for k in range(2):
-            nc.vector.tensor_copy(xs_picked[:, halves[k]], xs[:].indirect(l_offs[:, list_halves[k]]))
-        deal(nc, w1s_dealt[:], w1s[:])
-        for k in range(2):
-            nc.vector.tensor_copy(xw_picked[:, halves[k]], xw[:].indirect(l_offs[:, list_halves[k]]))
-
-        def banks(name):
-            return [
-                [psum.tile([P, S // 2], F32, name="%s%d_%d" % (name, t, k), tag="bank%d_%d" % (t, k)) for k in range(2)]
-                for t in range(PACK)
-            ]
+            nc.vector.tensor_copy(xs_picked[:, HALVES[k]], xs[:].indirect(l_offs[:, LIST_HALVES[k]]))
+        nc.vector.tensor_copy(xw_picked[:, HALVES[0]], xw[:].indirect(l_offs[:, LIST_HALVES[0]]))
+        deal(nc, w1s_dealt[:], ws[:])
+        nc.vector.tensor_copy(xw_picked[:, HALVES[1]], xw[:].indirect(l_offs[:, LIST_HALVES[1]]))
 
         y_bank = banks("y")
-        for t in range(PACK):
-            cols = slice(t * P, (t + 1) * P)
+        for t in range(PLANES):
+            rows = slice(t * P, (t + 1) * P)
             for k in range(2):
                 nc.tensor.matmul_mx(
-                    out=y_bank[t][k][:], lhsT=w1w_dealt[:, cols].bitcast(FP8X4), lhsT_scale=w1s_dealt[:, cols],
-                    rhs=xw_picked[:, halves[k]].bitcast(FP8X4), rhs_scale=xs_picked[:, halves[k]],
+                    out=y_bank[t][k][:], lhsT=w1w_dealt[:, rows].bitcast(FP8X4), lhsT_scale=w1s_dealt[W1_ROW:, rows],
+                    rhs=xw_picked[:, HALVES[k]].bitcast(FP8X4), rhs_scale=xs_picked[:, HALVES[k]],
                     start=True, stop=True,
                 )
 
@@ -125,156 +132,148 @@ def tile_picked_joinhopptrimpagez_none_po_kernel(
         w2w_dealt = w23w_dealt[:, :N]
         w3w_dealt = w23w_dealt[:, N:]
         w23s_dealt = sb("w23s_dealt", [P, N], U8)
-        w23w = keep.tile([P, 2 * N], I32, name="w23w", tag="w_raw", align_bytes=64)
-        load_words(nc.sync, w23w[:, :N], w2_words)
-        load_words(nc.sync, w23w[:, N:], w3_words)
-        load_scales([nc.sync] * 4, w1s, 4, w2_scales)
-        load_scales([nc.sync] * 4, w1s, 8, w3_scales)
+        w23w = sb("w23w", [P, 2 * N], I32, tag="w_raw")
+        load_words(nc, w23w[:, :N], w2_words)
+        load_words(nc, w23w[:, N:], w3_words)
+        load_scales(nc, ws, W2_ROW, w2_scales)
+        load_scales(nc, ws, W3_ROW, w3_scales)
         deal(nc, w2w_dealt, w23w[:, :N])
         deal(nc, w3w_dealt, w23w[:, N:])
-        deal(nc, w23s_dealt[:], w1s[:])
+        deal(nc, w23s_dealt[:], ws[:])
 
-        st4 = sb("st4", [P, PACK, S], F32)
-        sig4 = sb("sig4", [P, PACK, S], F32)
-        tanh4 = sb("tanh4", [P, PACK, S], F32)
-        a4 = sb("a4", [P, PACK, S], F32)
-        b4 = sb("b4", [P, PACK, S], F32)
-        m4 = sb("m4", [P, PACK, S], F32)
-        z_bf = sb("z_bf", [P, PACK * S], BF16)
-        z2_bf = sb("z2_bf", [P, PACK * S], BF16)
+        st_planes = sb("st_planes", [P, PLANES, S], F32)
+        sigmoid_planes = sb("sigmoid_planes", [P, PLANES, S], F32)
+        gate_planes = sb("gate_planes", [P, PLANES, S], F32)
+        d4_planes = sb("d4_planes", [P, PLANES, S], F32)
+        d5_planes = sb("d5_planes", [P, PLANES, S], F32)
+        max_planes = sb("max_planes", [P, PLANES, S], F32)
+        z_bf = sb("z_bf", [P, PLANES * S], BF16)
+        z2_bf = sb("z2_bf", [P, PLANES * S], BF16)
 
-        def leave_y(t):
-            for k in range(2):
-                nc.scalar.copy(y_slot[t][:, :S][:, halves[k]], y_bank[t][k][:])
-                nc.scalar.copy(y_slot[t + 1][:, S:][:, halves[k]], y_bank[t][k][:])
+        def make_u(t):
+            nc.vector.tensor_tensor(st_tile[t + 1][:, S:], y_tile[t][:].indirect(l3[:]), y_tile[t + 1][:, S:], ALU.add)
 
-        def first_sum(t):
-            nc.vector.tensor_tensor(st_slot[t + 1][:, S:], y_slot[t][:].indirect(l3[:]), y_slot[t + 1][:, S:], ALU.add)
-
-        def gated_sum(t):
-            nc.vector.tensor_tensor(st_slot[t][:, :S], y_slot[t][:].indirect(l1[:]), y_slot[t + 1][:, S:], ALU.add)
-            nc.sync.dma_start(out=st4[:, t, :], in_=st_slot[t][:, :S])
-            nc.scalar.activation(sig4[:, t, :], st_slot[t][:].indirect(l2[:]), ACT.Sigmoid, scale=2.0)
+        def make_st_and_gate(t):
+            nc.vector.tensor_tensor(st_tile[t][:, :S], y_tile[t][:].indirect(l1[:]), y_tile[t + 1][:, S:], ALU.add)
+            nc.sync.dma_start(out=st_planes[:, t, :], in_=st_tile[t][:, :S])
+            nc.scalar.activation(sigmoid_planes[:, t, :], st_tile[t][:].indirect(l2[:]), ACT.Sigmoid, scale=2.0)
             nc.scalar.activation(
-                tanh4[:, t, :], sig4[:, t, :], ACT.Identity, scale=gn_twice[:, t : t + 1], bias=gn_neg[:, t : t + 1]
+                gate_planes[:, t, :], sigmoid_planes[:, t, :], ACT.Identity,
+                scale=gn_twice[:, t : t + 1], bias=gn_neg[:, t : t + 1],
             )
 
-        def larger(t):
-            nc.vector.tensor_tensor(m4[:, t, :], a4[:, t, :], b4[:, t, :], ALU.max)
+        def make_z2(t):
+            nc.vector.tensor_tensor(max_planes[:, t, :], d4_planes[:, t, :], d5_planes[:, t, :], ALU.max)
+            plane = z2_bf[:].rearrange("p (j t) -> p t j", t=PLANES)[:, t, :]
+            for half in HALVES:
+                nc.scalar.activation(plane[:, half], max_planes[:, t, half], ACT.Copy, scale=gm_neg[:, t : t + 1])
 
-        def round_z2(t):
-            plane = z2_bf[:].rearrange("p (j t) -> p t j", t=PACK)[:, t, :]
-            for k in range(2):
-                nc.scalar.activation(
-                    plane[:, halves[k]], m4[:, t, halves[k]], ACT.Copy, scale=gm_neg[:, t : t + 1]
-                )
-
-        def product_z(c0, c1):
+        def make_z(half):
+            pairs = slice(half.start // 2, half.stop // 2)
             nc.vector.tensor_tensor(
-                z_bf[:].rearrange("p (c i t) -> p c t i", i=2, t=PACK)[:, c0:c1],
-                tanh4[:].rearrange("p t (c i) -> p c t i", i=2)[:, c0:c1],
-                st4[:].rearrange("p t (c i) -> p c t i", i=2)[:, c0:c1],
+                z_bf[:].rearrange("p (c i t) -> p c t i", i=2, t=PLANES)[:, pairs],
+                gate_planes[:].rearrange("p t (c i) -> p c t i", i=2)[:, pairs],
+                st_planes[:].rearrange("p t (c i) -> p c t i", i=2)[:, pairs],
                 ALU.mult,
             )
 
-        for t in range(PACK):
-            leave_y(t)
-        gated_sum(0)
-        first_sum(0)
-        for t in range(PACK):
-            window = y_slot[t][:]
-            u = st_slot[t + 1][:, S:]
-            if t + 1 < PACK:
-                gated_sum(t + 1)
-            nc.vector.tensor_tensor(a4[:, t, :], window.indirect(l4[:]), u, ALU.subtract)
-            nc.vector.tensor_tensor(b4[:, t, :], window.indirect(l5[:]), u, ALU.subtract)
-            if t + 1 < PACK:
-                first_sum(t + 1)
-            else:
-                product_z(0, S // 4)
-            larger(t)
-            round_z2(t)
-        product_z(S // 4, S // 2)
+        for t in range(PLANES):
+            for k in range(2):
+                nc.scalar.copy(y_tile[t][:, :S][:, HALVES[k]], y_bank[t][k][:])
+                nc.scalar.copy(y_tile[t + 1][:, S:][:, HALVES[k]], y_bank[t][k][:])
 
-        page_tags = ["xw_picked", "xs", "w_raw", "w1s"]
-        page = [sb("page%d" % t, [P, U], F32, tag=page_tags[t]) for t in range(PACK)]
-        h_slot = [sb("h_slot%d" % t, [P, 2 * S], F32, tag="y_slot%d" % t) for t in range(PACK + 1)]
-        minus_one = sb("minus_one", [P, S], F32, tag="w1w_dealt")
-        nc.gpsimd.memset(h_slot[0][:, S:], 0.0)
-        nc.gpsimd.memset(minus_one[:], -1.0)
-        for t in range(PACK):
-            nc.gpsimd.memset(page[t][:], 0.0)
+        make_st_and_gate(0)
+        make_u(0)
+        for t in range(PLANES):
+            window = y_tile[t][:]
+            u = st_tile[t + 1][:, S:]
+            last = t + 1 == PLANES
+            if not last:
+                make_st_and_gate(t + 1)
+            nc.vector.tensor_tensor(d4_planes[:, t, :], window.indirect(l4[:]), u, ALU.subtract)
+            nc.vector.tensor_tensor(d5_planes[:, t, :], window.indirect(l5[:]), u, ALU.subtract)
+            if last:
+                make_z(HALVES[0])
+            else:
+                make_u(t + 1)
+            make_z2(t)
+        make_z(HALVES[1])
 
         z_codes = sb("z_codes", [P, S], U32)
         z_scales = sb("z_scales", [P, S], U8)
         z2_codes = sb("z2_codes", [P, S], U32)
         z2_scales = sb("z2_scales", [P, S], U8)
-        for k in range(2):
-            wide = slice(PACK * halves[k].start, PACK * halves[k].stop)
+        for half in HALVES:
+            elements = slice(PLANES * half.start, PLANES * half.stop)
+            nc.vector.quantize_mx(out=z_codes[:, half].bitcast(FP8X4), scales=z_scales[:, half], in_=z_bf[:, elements])
             nc.vector.quantize_mx(
-                out=z_codes[:, halves[k]].bitcast(FP8X4), scales=z_scales[:, halves[k]], in_=z_bf[:, wide]
-            )
-            nc.vector.quantize_mx(
-                out=z2_codes[:, halves[k]].bitcast(FP8X4), scales=z2_scales[:, halves[k]], in_=z2_bf[:, wide]
+                out=z2_codes[:, half].bitcast(FP8X4), scales=z2_scales[:, half], in_=z2_bf[:, elements]
             )
 
+        late_pages = [sb("page0", [P, U], F32, tag="z_bf"), sb("page1", [P, U], F32, tag="z2_bf")]
+        for tile in late_pages:
+            nc.vector.memset(tile[:], 0.0)
+        page = late_pages + early_pages
+
         h_bank = banks("h")
-        for t in range(PACK):
-            cols = slice(t * P, (t + 1) * P)
+        for t in range(PLANES):
+            rows = slice(t * P, (t + 1) * P)
             for k in range(2):
                 nc.tensor.matmul_mx(
-                    out=h_bank[t][k][:], lhsT=w2w_dealt[:, cols].bitcast(FP8X4), lhsT_scale=w23s_dealt[4:, cols],
-                    rhs=z_codes[:, halves[k]].bitcast(FP8X4), rhs_scale=z_scales[:, halves[k]],
+                    out=h_bank[t][k][:], lhsT=w2w_dealt[:, rows].bitcast(FP8X4), lhsT_scale=w23s_dealt[W2_ROW:, rows],
+                    rhs=z_codes[:, HALVES[k]].bitcast(FP8X4), rhs_scale=z_scales[:, HALVES[k]],
                     start=True, stop=False,
                 )
                 nc.tensor.matmul_mx(
-                    out=h_bank[t][k][:], lhsT=w3w_dealt[:, cols].bitcast(FP8X4), lhsT_scale=w23s_dealt[8:, cols],
-                    rhs=z2_codes[:, halves[k]].bitcast(FP8X4), rhs_scale=z2_scales[:, halves[k]],
+                    out=h_bank[t][k][:], lhsT=w3w_dealt[:, rows].bitcast(FP8X4), lhsT_scale=w23s_dealt[W3_ROW:, rows],
+                    rhs=z2_codes[:, HALVES[k]].bitcast(FP8X4), rhs_scale=z2_scales[:, HALVES[k]],
                     start=False, stop=True,
                 )
 
-        nw_neg = sb("nw_neg", [P, PACK, S], F32)
-        page_bf = sb("page_bf", [P, PACK * U], BF16)
+        nw_neg = sb("nw_neg", [P, PLANES, S], F32)
+        page_bf = sb("page_bf", [P, PLANES * U], BF16)
         page_codes = sb("page_codes", [P, U], U32)
         page_scales = sb("page_scales", [P, U], U8)
-        rows = out_0.rearrange("(p t) c -> p t c", t=PACK)
-        planes = page_bf[:].rearrange("p (c t) -> p t c", t=PACK)
-        by_column = page_bf[:].rearrange("p (c t) -> p c t", t=PACK)
+        out_planes = out_0.rearrange("(p t) c -> p t c", t=PLANES)
+        bf_planes = page_bf[:].rearrange("p (c t) -> p t c", t=PLANES)
+        bf_columns = page_bf[:].rearrange("p (c t) -> p c t", t=PLANES)
 
-        for t in range(PACK):
+        for t in range(PLANES):
             for k in range(2):
-                nc.scalar.activation(h_slot[t][:, :S][:, halves[k]], h_bank[t][k][:], ACT.Relu)
-                nc.scalar.copy(h_slot[t + 1][:, S:][:, halves[k]], h_bank[t][k][:])
+                nc.scalar.activation(y_tile[t][:, :S][:, HALVES[k]], h_bank[t][k][:], ACT.Relu)
+                nc.scalar.copy(y_tile[t + 1][:, S:][:, HALVES[k]], h_bank[t][k][:])
 
-        pieces = [slice(0, HALF), slice(HALF, HALF + U // 4), slice(HALF + U // 4, U)]
+        def make_nw_neg(t):
+            nc.vector.tensor_tensor(nw_neg[:, t, :], y_tile[t][:].indirect(l7[:]), y_tile[t + 1][:, S:], ALU.subtract)
 
-        def look_up_h(t):
-            nc.vector.tensor_tensor(nw_neg[:, t, :], h_slot[t][:].indirect(l7[:]), h_slot[t + 1][:, S:], ALU.subtract)
-
-        for t in range(PACK):
-            if t != 2:
-                look_up_h(t)
-            if t == 1:
-                look_up_h(2)
-            nc.vector.tensor_tensor(page[t][:].indirect(l6[:]), nw_neg[:, t, :], minus_one[:], ALU.mult)
-            nc.sync.dma_start(out=rows[:, t, :], in_=page[t][:])
-            if t < 2:
-                nc.scalar.copy(planes[:, t, :], page[t][:])
-            elif t == 2:
-                nc.scalar.copy(by_column[:, :, 2:], page[t][:].unsqueeze(2).to_broadcast([P, U, 2]))
+        def round_plane(t):
+            if t < PLANES - 2:
+                nc.scalar.copy(bf_planes[:, t, :], page[t][:])
+            elif t == PLANES - 2:
+                for cols in (PIECES[0], slice(PIECES[0].stop, U)):
+                    width = cols.stop - cols.start
+                    nc.scalar.copy(bf_columns[:, cols, t:], page[t][:, cols].unsqueeze(2).to_broadcast([P, width, 2]))
             else:
-                nc.vector.tensor_copy(planes[:, t, :HALF], page[t][:, :HALF])
-                for cols in pieces[1:]:
-                    nc.scalar.copy(planes[:, t, cols], page[t][:, cols])
+                nc.vector.tensor_copy(bf_planes[:, t, PIECES[0]], page[t][:, PIECES[0]])
+                for cols in PIECES[1:]:
+                    nc.scalar.copy(bf_planes[:, t, cols], page[t][:, cols])
 
-        words = out_1[0].rearrange("p c r -> p (c r)").bitcast(I32)
-        for cols in pieces:
+        make_nw_neg(0)
+        for t in range(PLANES):
+            if t + 1 < PLANES:
+                make_nw_neg(t + 1)
+            nc.vector.tensor_tensor(page[t][:].indirect(l6[:]), nw_neg[:, t, :], minus_one, ALU.mult)
+            nc.sync.dma_start(out=out_planes[:, t, :], in_=page[t][:])
+            round_plane(t)
+
+        out_words = out_1[0].rearrange("p c r -> p (c r)").bitcast(I32)
+        for cols in PIECES:
             nc.vector.quantize_mx(
                 out=page_codes[:, cols].bitcast(FP8X4), scales=page_scales[:, cols],
-                in_=page_bf[:, PACK * cols.start : PACK * cols.stop],
+                in_=page_bf[:, PLANES * cols.start : PLANES * cols.stop],
             )
-            nc.sync.dma_start(out=words[:, cols], in_=page_codes[:, cols].bitcast(I32))
-        for q in range(4):
+            nc.sync.dma_start(out=out_words[:, cols], in_=page_codes[:, cols].bitcast(I32))
+        for q in range(QUADRANTS):
             queue = nc.scalar if q % 2 == 0 else nc.sync
             queue.dma_start(
                 out=out_2[0, 4 * q : 4 * q + 4, :].bitcast(I32), in_=page_scales[32 * q : 32 * q + 4, :].bitcast(I32)

from contextlib import ExitStack

import concourse.mybir as mybir

T, S, N, H, U = 2048, 512, 512, 512, 1024
FLOPS = 3 * 2 * 512 * 512 * 512

F32 = mybir.dt.float32
BF16 = mybir.dt.bfloat16
I32 = mybir.dt.int32
U32 = mybir.dt.uint32
U16 = mybir.dt.uint16
U8 = mybir.dt.uint8
FP8X4 = mybir.dt.float8_e4m3fn_x4
ALU = mybir.AluOpType
ACT = mybir.ActivationFunctionType

P = 128
PLANES = 4
QUADRANTS = 4
W1_ROW, W2_ROW, W3_ROW = 0, 4, 8

HALVES = [slice(0, S // 2), slice(S // 2, S)]
LIST_HALVES = [slice(0, S // 32), slice(S // 32, S // 16)]

PIECES = [slice(0, U // 2), slice(U // 2, 3 * U // 4), slice(3 * U // 4, U)]


def load_words(nc, words_sb, words):
    nc.sync.dma_start(out=words_sb.bitcast(I32), in_=words[0].rearrange("p c r -> p (c r)").bitcast(I32))


def load_scales(nc, tile, first_row, scales):
    for q in range(QUADRANTS):
        row = 32 * q + first_row
        nc.sync.dma_start(out=tile[row : row + 4, :].bitcast(I32), in_=scales[0, 4 * q : 4 * q + 4, :].bitcast(I32))


def deal(nc, dealt, raw):
    nc.vector.tensor_copy(
        out=dealt.rearrange("p (t m) -> p t m", t=PLANES), in_=raw.rearrange("p (m t) -> p t m", t=PLANES)
    )


def tile_picked_joinhopptrimpagez_none_po_kernel(
    tc, x_words, x_scales, w1_words, w1_scales, gn, gm, w2_words, w2_scales, w3_words, w3_scales,
    offs, n1, n2, n3, n4, n5, n6, n7, out_0, out_1, out_2,
):
    nc = tc.nc
    with ExitStack() as ctx:
        lists = ctx.enter_context(tc.tile_pool(name="lists", bufs=1))
        keep = ctx.enter_context(tc.tile_pool(name="keep", bufs=1))
        psum = ctx.enter_context(tc.psum_pool(name="psum", bufs=1))

        def sb(name, shape, dtype, tag=None):
            return keep.tile(shape, dtype, name=name, tag=tag or name, align_bytes=64)

        def load_list(name, src):
            tile = lists.tile([P, S // 16], U16, name=name)
            nc.sync.dma_start(tile[:], src)
            return tile

        def banks(name):
            return [
                [psum.tile([P, S // 2], F32, name="%s%d_%d" % (name, t, k), tag="bank%d_%d" % (t, k)) for k in range(2)]
                for t in range(PLANES)
            ]

        xw = sb("xw", [P, T], U32)
        xs = sb("xs", [P, T], U8)
        w1w = sb("w1w", [P, H], I32, tag="w_raw")
        ws = sb("ws", [P, H], U8)
        nc.vector.memset(xs[:].bitcast(I32), 0)
        nc.vector.memset(ws[:].bitcast(I32), 0)
        gn_sb = sb("gn_sb", [P, PLANES], F32)
        gm_sb = sb("gm_sb", [P, PLANES], F32)

        l_offs = load_list("l_offs", offs)
        l1 = load_list("l1", n1)
        load_words(nc, w1w[:], w1_words)
        load_scales(nc, xs, 0, x_scales)
        l3 = load_list("l3", n3)
        l4 = load_list("l4", n4)
        load_words(nc, xw[:], x_words)
        load_scales(nc, ws, W1_ROW, w1_scales)
        l5 = load_list("l5", n5)
        l2 = load_list("l2", n2)
        nc.sync.dma_start(out=gn_sb[:], in_=gn.rearrange("(p t) o -> p (t o)", t=PLANES))
        nc.sync.dma_start(out=gm_sb[:], in_=gm.rearrange("(p t) o -> p (t o)", t=PLANES))
        l7 = load_list("l7", n7)
        l6 = load_list("l6", n6)

        y_tile = [sb("y_tile%d" % t, [P, 2 * S], F32) for t in range(PLANES + 1)]
        st_tile = [sb("st_tile%d" % t, [P, 2 * S], F32) for t in range(PLANES + 1)]
        minus_one = y_tile[0][:, S:]
        nc.vector.memset(minus_one, -1.0)
        nc.vector.memset(st_tile[0][:, S:], 0.0)

        early_pages = [sb("page%d" % t, [P, U], F32) for t in (2, 3)]
        for tile in early_pages:
            nc.vector.memset(tile[:], 0.0)

        gn_twice = sb("gn_twice", [P, PLANES], F32)
        gn_neg = sb("gn_neg", [P, PLANES], F32)
        gm_neg = sb("gm_neg", [P, PLANES], F32)
        nc.scalar.mul(gn_twice[:], gn_sb[:], 2.0)
        nc.scalar.mul(gn_neg[:], gn_sb[:], -1.0)
        nc.scalar.mul(gm_neg[:], gm_sb[:], -1.0)

        xs_picked = sb("xs_picked", [P, S], U8)
        xw_picked = sb("xw_picked", [P, S], U32)
        w1w_dealt = sb("w1w_dealt", [P, H], I32)
        w1s_dealt = sb("w1s_dealt", [P, H], U8)
        deal(nc, w1w_dealt[:], w1w[:])
        for k in range(2):
            nc.vector.tensor_copy(xs_picked[:, HALVES[k]], xs[:].indirect(l_offs[:, LIST_HALVES[k]]))
        nc.vector.tensor_copy(xw_picked[:, HALVES[0]], xw[:].indirect(l_offs[:, LIST_HALVES[0]]))
        deal(nc, w1s_dealt[:], ws[:])
        nc.vector.tensor_copy(xw_picked[:, HALVES[1]], xw[:].indirect(l_offs[:, LIST_HALVES[1]]))

        y_bank = banks("y")
        for t in range(PLANES):
            rows = slice(t * P, (t + 1) * P)
            for k in range(2):
                nc.tensor.matmul_mx(
                    out=y_bank[t][k][:], lhsT=w1w_dealt[:, rows].bitcast(FP8X4), lhsT_scale=w1s_dealt[W1_ROW:, rows],
                    rhs=xw_picked[:, HALVES[k]].bitcast(FP8X4), rhs_scale=xs_picked[:, HALVES[k]],
                    start=True, stop=True,
                )

        w23w_dealt = sb("w23w_dealt", [P, 2 * N], I32, tag="xw")
        w2w_dealt = w23w_dealt[:, :N]
        w3w_dealt = w23w_dealt[:, N:]
        w23s_dealt = sb("w23s_dealt", [P, N], U8)
        w23w = sb("w23w", [P, 2 * N], I32, tag="w_raw")
        load_words(nc, w23w[:, :N], w2_words)
        load_words(nc, w23w[:, N:], w3_words)
        load_scales(nc, ws, W2_ROW, w2_scales)
        load_scales(nc, ws, W3_ROW, w3_scales)
        deal(nc, w2w_dealt, w23w[:, :N])
        deal(nc, w3w_dealt, w23w[:, N:])
        deal(nc, w23s_dealt[:], ws[:])

        st_planes = sb("st_planes", [P, PLANES, S], F32)
        sigmoid_planes = sb("sigmoid_planes", [P, PLANES, S], F32)
        gate_planes = sb("gate_planes", [P, PLANES, S], F32)
        d4_planes = sb("d4_planes", [P, PLANES, S], F32)
        d5_planes = sb("d5_planes", [P, PLANES, S], F32)
        max_planes = sb("max_planes", [P, PLANES, S], F32)
        z_bf = sb("z_bf", [P, PLANES * S], BF16)
        z2_bf = sb("z2_bf", [P, PLANES * S], BF16)

        def make_u(t):
            nc.vector.tensor_tensor(st_tile[t + 1][:, S:], y_tile[t][:].indirect(l3[:]), y_tile[t + 1][:, S:], ALU.add)

        def make_st_and_gate(t):
            nc.vector.tensor_tensor(st_tile[t][:, :S], y_tile[t][:].indirect(l1[:]), y_tile[t + 1][:, S:], ALU.add)
            nc.sync.dma_start(out=st_planes[:, t, :], in_=st_tile[t][:, :S])
            nc.scalar.activation(sigmoid_planes[:, t, :], st_tile[t][:].indirect(l2[:]), ACT.Sigmoid, scale=2.0)
            nc.scalar.activation(
                gate_planes[:, t, :], sigmoid_planes[:, t, :], ACT.Identity,
                scale=gn_twice[:, t : t + 1], bias=gn_neg[:, t : t + 1],
            )

        def make_z2(t):
            nc.vector.tensor_tensor(max_planes[:, t, :], d4_planes[:, t, :], d5_planes[:, t, :], ALU.max)
            plane = z2_bf[:].rearrange("p (j t) -> p t j", t=PLANES)[:, t, :]
            for half in HALVES:
                nc.scalar.activation(plane[:, half], max_planes[:, t, half], ACT.Copy, scale=gm_neg[:, t : t + 1])

        def make_z(half):
            pairs = slice(half.start // 2, half.stop // 2)
            nc.vector.tensor_tensor(
                z_bf[:].rearrange("p (c i t) -> p c t i", i=2, t=PLANES)[:, pairs],
                gate_planes[:].rearrange("p t (c i) -> p c t i", i=2)[:, pairs],
                st_planes[:].rearrange("p t (c i) -> p c t i", i=2)[:, pairs],
                ALU.mult,
            )

        for t in range(PLANES):
            for k in range(2):
                nc.scalar.copy(y_tile[t][:, :S][:, HALVES[k]], y_bank[t][k][:])
                nc.scalar.copy(y_tile[t + 1][:, S:][:, HALVES[k]], y_bank[t][k][:])

        make_st_and_gate(0)
        make_u(0)
        for t in range(PLANES):
            window = y_tile[t][:]
            u = st_tile[t + 1][:, S:]
            last = t + 1 == PLANES
            if not last:
                make_st_and_gate(t + 1)
            nc.vector.tensor_tensor(d4_planes[:, t, :], window.indirect(l4[:]), u, ALU.subtract)
            nc.vector.tensor_tensor(d5_planes[:, t, :], window.indirect(l5[:]), u, ALU.subtract)
            if last:
                make_z(HALVES[0])
            else:
                make_u(t + 1)
            make_z2(t)
        make_z(HALVES[1])

        z_codes = sb("z_codes", [P, S], U32)
        z_scales = sb("z_scales", [P, S], U8)
        z2_codes = sb("z2_codes", [P, S], U32)
        z2_scales = sb("z2_scales", [P, S], U8)
        for half in HALVES:
            elements = slice(PLANES * half.start, PLANES * half.stop)
            nc.vector.quantize_mx(out=z_codes[:, half].bitcast(FP8X4), scales=z_scales[:, half], in_=z_bf[:, elements])
            nc.vector.quantize_mx(
                out=z2_codes[:, half].bitcast(FP8X4), scales=z2_scales[:, half], in_=z2_bf[:, elements]
            )

        late_pages = [sb("page0", [P, U], F32, tag="z_bf"), sb("page1", [P, U], F32, tag="z2_bf")]
        for tile in late_pages:
            nc.vector.memset(tile[:], 0.0)
        page = late_pages + early_pages

        h_bank = banks("h")
        for t in range(PLANES):
            rows = slice(t * P, (t + 1) * P)
            for k in range(2):
                nc.tensor.matmul_mx(
                    out=h_bank[t][k][:], lhsT=w2w_dealt[:, rows].bitcast(FP8X4), lhsT_scale=w23s_dealt[W2_ROW:, rows],
                    rhs=z_codes[:, HALVES[k]].bitcast(FP8X4), rhs_scale=z_scales[:, HALVES[k]],
                    start=True, stop=False,
                )
                nc.tensor.matmul_mx(
                    out=h_bank[t][k][:], lhsT=w3w_dealt[:, rows].bitcast(FP8X4), lhsT_scale=w23s_dealt[W3_ROW:, rows],
                    rhs=z2_codes[:, HALVES[k]].bitcast(FP8X4), rhs_scale=z2_scales[:, HALVES[k]],
                    start=False, stop=True,
                )

        nw_neg = sb("nw_neg", [P, PLANES, S], F32)
        page_bf = sb("page_bf", [P, PLANES * U], BF16)
        page_codes = sb("page_codes", [P, U], U32)
        page_scales = sb("page_scales", [P, U], U8)
        out_planes = out_0.rearrange("(p t) c -> p t c", t=PLANES)
        bf_planes = page_bf[:].rearrange("p (c t) -> p t c", t=PLANES)
        bf_columns = page_bf[:].rearrange("p (c t) -> p c t", t=PLANES)

        for t in range(PLANES):
            for k in range(2):
                nc.scalar.activation(y_tile[t][:, :S][:, HALVES[k]], h_bank[t][k][:], ACT.Relu)
                nc.scalar.copy(y_tile[t + 1][:, S:][:, HALVES[k]], h_bank[t][k][:])

        def make_nw_neg(t):
            nc.vector.tensor_tensor(nw_neg[:, t, :], y_tile[t][:].indirect(l7[:]), y_tile[t + 1][:, S:], ALU.subtract)

        def round_plane(t):
            if t < PLANES - 2:
                nc.scalar.copy(bf_planes[:, t, :], page[t][:])
            elif t == PLANES - 2:
                for cols in (PIECES[0], slice(PIECES[0].stop, U)):
                    width = cols.stop - cols.start
                    nc.scalar.copy(bf_columns[:, cols, t:], page[t][:, cols].unsqueeze(2).to_broadcast([P, width, 2]))
            else:
                nc.vector.tensor_copy(bf_planes[:, t, PIECES[0]], page[t][:, PIECES[0]])
                for cols in PIECES[1:]:
                    nc.scalar.copy(bf_planes[:, t, cols], page[t][:, cols])

        make_nw_neg(0)
        for t in range(PLANES):
            if t + 1 < PLANES:
                make_nw_neg(t + 1)
            nc.vector.tensor_tensor(page[t][:].indirect(l6[:]), nw_neg[:, t, :], minus_one, ALU.mult)
            nc.sync.dma_start(out=out_planes[:, t, :], in_=page[t][:])
            round_plane(t)

        out_words = out_1[0].rearrange("p c r -> p (c r)").bitcast(I32)
        for cols in PIECES:
            nc.vector.quantize_mx(
                out=page_codes[:, cols].bitcast(FP8X4), scales=page_scales[:, cols],
                in_=page_bf[:, PLANES * cols.start : PLANES * cols.stop],
            )
            nc.sync.dma_start(out=out_words[:, cols], in_=page_codes[:, cols].bitcast(I32))
        for q in range(QUADRANTS):
            queue = nc.scalar if q % 2 == 0 else nc.sync
            queue.dma_start(
                out=out_2[0, 4 * q : 4 * q + 4, :].bitcast(I32), in_=page_scales[32 * q : 32 * q + 4, :].bitcast(I32)
            )
